import numpy as np
import ml_dtypes


def mxq(x, axis, fmt="e4m3"):
    dtype, down = {"e4m3": (ml_dtypes.float8_e4m3fn, 7), "e5m2": (ml_dtypes.float8_e5m2, 14)}[fmt]
    v = np.moveaxis(np.asarray(x, np.float32).astype(ml_dtypes.bfloat16).astype(np.float64), axis, -1)
    blocks = v.reshape(v.shape[:-1] + (-1, 32))
    amax = np.abs(blocks).max(-1, keepdims=True)
    byte = np.maximum(np.where(amax > 0, np.frexp(amax)[1] - 1 + 127, 0) - down, 1)
    scale = np.exp2(byte - 127.0)
    codes = (blocks / scale).astype(np.float32).astype(dtype).astype(np.float64)
    return np.moveaxis((codes * scale).reshape(v.shape), -1, axis)


WIDE = False


def mx_kscale(k):
    if not WIDE:
        return np.ones(k)
    levels = np.array([10, -10, 5, -5, 0])
    if k % 512:
        return np.exp2(np.random.permutation(np.resize(levels, k // 32))).repeat(32)
    a = np.empty((k // 512, 16))
    for p in range(k // 512):
        a[p, :8] = np.random.permutation(np.resize(levels, 8))
        for g in range(8):
            far = levels[np.abs(levels - a[p, g]) >= 10]
            a[p, g + 8] = far[np.random.randint(len(far))]
    return np.exp2(a.ravel()).repeat(32)


def f64(x):
    return np.asarray(x).astype(np.float64)


def striped(idx):
    return np.tile(idx.reshape(-1, 16).T, (8, 1)).astype(np.uint16)


def unstriped(offs):
    return offs[:16].T.reshape(-1).astype(np.int64)


def pack_weight(w):
    k, n = w.shape
    w = f64(np.asarray(w, np.float32).astype(ml_dtypes.bfloat16)).reshape(k // 32, 32, n)
    amax = np.abs(w).max(1)
    byte = np.clip(np.where(amax > 0, np.frexp(amax)[1] - 1 + 127 - 7, 1), 1, 254)
    scaled = (w * np.exp2(127.0 - byte)[:, None, :]).reshape(k, n).astype(np.float32)
    words = np.ascontiguousarray(scaled.reshape(k // 512, 128, 4, n).transpose(0, 1, 3, 2)).astype(ml_dtypes.float8_e4m3fn).view(np.uint8)
    return words, np.ascontiguousarray(byte.astype(np.uint8).reshape(k // 512, 16, n))


def unpack_weight(words, scales):
    g, p, n, _ = words.shape
    vals = np.ascontiguousarray(words).view(ml_dtypes.float8_e4m3fn).astype(np.float64) * np.repeat(np.exp2(scales.astype(np.float64) - 127.0), 8, axis=1)[..., None]
    return vals.transpose(0, 1, 3, 2).reshape(g * 512, n)


K, T, N = 512, 512, 256


def setup_inputs():
    n = np.random.standard_normal
    s = mx_kscale(K)[:, None]
    packed_xT = pack_weight(n((K, T)) * s)
    return {
        "x_words": packed_xT[0],
        "x_scales": packed_xT[1],
        "w1": (n((K, N)) / np.sqrt(K) / s).astype(np.float32),
        "pos1": striped(np.random.permutation(T)),
        "pos2": striped(np.random.permutation(T)),
        "pos3": striped(np.random.permutation(T)),
    }


def reference(x_words, x_scales, w1, pos1, pos2, pos3):
    xq = unpack_weight(x_words, x_scales)
    y = mxq(f64(w1), 0, "e4m3").T @ xq
    n0 = y[:, unstriped(pos1)]
    n1 = y[:, unstriped(pos2)]
    n2 = y[:, unstriped(pos3)]
    return np.maximum(np.minimum(n0, n1), np.minimum(np.maximum(n0, n1), n2))

@@ -1,0 +1,103 @@
+from contextlib import ExitStack
+
+import concourse.mybir as mybir
+
+K, T, N = 512, 512, 256
+FLOPS = 2 * K * T * N
+
+F32 = mybir.dt.float32
+BF16 = mybir.dt.bfloat16
+I32 = mybir.dt.int32
+U32 = mybir.dt.uint32
+U16 = mybir.dt.uint16
+U8 = mybir.dt.uint8
+FP8X4 = mybir.dt.float8_e4m3fn_x4
+MAX = mybir.AluOpType.max
+MIN = mybir.AluOpType.min
+
+P = 128
+PACK = 4
+HALF = T // 2
+
+
+def tile_picked_wmedian_none_l_kernel(tc, x_words, x_scales, w1, pos1, pos2, pos3, out):
+    nc = tc.nc
+    with ExitStack() as ctx:
+        keep = ctx.enter_context(tc.tile_pool(name="keep", bufs=1))
+        psum = ctx.enter_context(tc.psum_pool(name="psum", bufs=1))
+
+        lists = [keep.tile([P, T // 16], U16, name=f"list{i}") for i in range(3)]
+        w_raw = [keep.tile([P, PACK, P], F32, name=f"w_raw{b}") for b in range(2)]
+        w_bf = [keep.tile([P, P, PACK], BF16, name=f"w_bf{b}", align_bytes=64) for b in range(2)]
+        w_codes = [keep.tile([P, P], U32, name=f"w_codes{b}", align_bytes=64) for b in range(2)]
+        w_sc = [keep.tile([P, P], U8, name=f"w_sc{b}", align_bytes=64) for b in range(2)]
+        x_codes = keep.tile([P, T], U32, name="x_codes", align_bytes=64)
+        x_sc = keep.tile([P, T], U8, name="x_sc", align_bytes=64)
+        y = [keep.tile([P, T], F32, name=f"y{b}") for b in range(2)]
+        picked = [[keep.tile([P, T], F32, name=f"n{b}_{i}") for i in range(3)] for b in range(2)]
+        hi = [keep.tile([P, T], F32, name=f"hi{b}") for b in range(2)]
+        lo = [keep.tile([P, T], F32, name=f"lo{b}") for b in range(2)]
+        cut = [keep.tile([P, T], F32, name=f"cut{b}") for b in range(2)]
+        med = [keep.tile([P, T], F32, name=f"med{b}") for b in range(2)]
+        acc = [[psum.tile([P, HALF], F32, name=f"acc{b}_{h}") for h in range(2)] for b in range(2)]
+
+        w_view = w1.rearrange("(p j) n -> p j n", j=PACK)
+        nc.vector.memset(x_sc[:].bitcast(U32), 0)
+        nc.sync.dma_start(out=w_raw[0][:], in_=w_view[:, :, 0:P])
+        for q in range(4):
+            nc.scalar.dma_start(out=x_sc[32 * q : 32 * q + 4, :].bitcast(I32), in_=x_scales[0, 4 * q : 4 * q + 4, :].bitcast(I32))
+        nc.sync.dma_start(out=x_codes[:].bitcast(I32), in_=x_words[0].rearrange("p n t -> p (n t)").bitcast(I32))
+        nc.sync.dma_start(lists[0][:], pos1)
+        nc.sync.dma_start(out=w_raw[1][:], in_=w_view[:, :, P : 2 * P])
+        nc.sync.dma_start(lists[1][:], pos2)
+        nc.sync.dma_start(lists[2][:], pos3)
+
+        def quantise(b):
+            nc.vector.quantize_mx(out=w_codes[b][:].bitcast(FP8X4), scales=w_sc[b][:], in_=w_bf[b][:].rearrange("p n j -> p (n j)"))
+
+        def project(b, h):
+            cols = slice(h * HALF, (h + 1) * HALF)
+            nc.tensor.matmul_mx(out=acc[b][h][:], lhsT=w_codes[b][:].bitcast(FP8X4), lhsT_scale=w_sc[b][:],
+                                rhs=x_codes[:, cols].bitcast(FP8X4), rhs_scale=x_sc[:, cols], start=True, stop=True)
+
+        def gather(b, i, h):
+            nc.vector.tensor_copy(picked[b][i][:, h * HALF : (h + 1) * HALF], y[b][:].indirect(lists[i][:, h * 16 : (h + 1) * 16]))
+
+        def op(dst, a, c, alu, lo_col, hi_col):
+            nc.vector.tensor_tensor(dst[:, lo_col:hi_col], a[:, lo_col:hi_col], c[:, lo_col:hi_col], alu)
+
+        nc.vector.tensor_copy(out=w_bf[0][:], in_=w_raw[0][:].rearrange("p j n -> p n j"))
+        quantise(0)
+        project(0, 0)
+        project(0, 1)
+        nc.scalar.copy(y[0][:, 0:HALF], acc[0][0][:])
+        nc.vector.tensor_copy(y[0][:, HALF:T], acc[0][1][:])
+        nc.scalar.copy(w_bf[1][:], w_raw[1][:].rearrange("p j n -> p n j"))
+        gather(0, 0, 0)
+        gather(0, 0, 1)
+        quantise(1)
+        project(1, 0)
+        project(1, 1)
+        nc.scalar.copy(y[1][:, 0:HALF], acc[1][0][:])
+        nc.scalar.copy(y[1][:, HALF:T], acc[1][1][:])
+        for i in (1, 2):
+            gather(0, i, 0)
+            gather(0, i, 1)
+        op(hi[0], picked[0][0], picked[0][1], MAX, 0, T)
+        op(lo[0], picked[0][0], picked[0][1], MIN, 0, T)
+        op(cut[0], hi[0], picked[0][2], MIN, 0, T)
+        gather(1, 0, 0)
+        op(med[0], lo[0], cut[0], MAX, 0, T)
+        nc.sync.dma_start(out=out[0:P, :], in_=med[0][:])
+        gather(1, 0, 1)
+        for i in (1, 2):
+            gather(1, i, 0)
+            gather(1, i, 1)
+        op(hi[1], picked[1][0], picked[1][1], MAX, 0, T)
+        op(lo[1], picked[1][0], picked[1][1], MIN, 0, T)
+        op(cut[1], hi[1], picked[1][2], MIN, 0, HALF)
+        op(cut[1], hi[1], picked[1][2], MIN, HALF, T)
+        op(med[1], lo[1], cut[1], MAX, 0, HALF)
+        nc.sync.dma_start(out=out[P : 2 * P, 0:HALF], in_=med[1][:, 0:HALF])
+        op(med[1], lo[1], cut[1], MAX, HALF, T)
+        nc.scalar.dma_start(out=out[P : 2 * P, HALF:T], in_=med[1][:, HALF:T])

@@ -28,8 +28,8 @@ def tile_picked_wmedian_none_l_kernel(tc, x_words, x_scales, w1, pos1, pos2, pos
 
         lists = [keep.tile([P, T // 16], U16, name=f"list{i}") for i in range(3)]
         w_raw = [keep.tile([P, PACK, P], F32, name=f"w_raw{b}") for b in range(2)]
-        w_bf = [keep.tile([P, P, PACK], BF16, name=f"w_bf{b}", align_bytes=64) for b in range(2)]
-        w_codes = [keep.tile([P, P], U32, name=f"w_codes{b}", align_bytes=64) for b in range(2)]
+        w_bf = [keep.tile([P, P, PACK], BF16, name="w_bf0", align_bytes=64)]
+        w_codes = [keep.tile([P, P], U32, name="w_codes0", tag="relay", align_bytes=64), keep.tile([P, P], U32, name="w_codes1", align_bytes=64)]
         w_sc = [keep.tile([P, P], U8, name=f"w_sc{b}", align_bytes=64) for b in range(2)]
         x_codes = keep.tile([P, T], U32, name="x_codes", align_bytes=64)
         x_sc = keep.tile([P, T], U8, name="x_sc", align_bytes=64)
@@ -42,10 +42,9 @@ def tile_picked_wmedian_none_l_kernel(tc, x_words, x_scales, w1, pos1, pos2, pos
         acc = [[psum.tile([P, HALF], F32, name=f"acc{b}_{h}") for h in range(2)] for b in range(2)]
 
         w_view = w1.rearrange("(p j) n -> p j n", j=PACK)
-        nc.vector.memset(x_sc[:].bitcast(U32), 0)
         nc.sync.dma_start(out=w_raw[0][:], in_=w_view[:, :, 0:P])
         for q in range(4):
-            nc.scalar.dma_start(out=x_sc[32 * q : 32 * q + 4, :].bitcast(I32), in_=x_scales[0, 4 * q : 4 * q + 4, :].bitcast(I32))
+            nc.sync.dma_start(out=x_sc[32 * q : 32 * q + 4, :].bitcast(I32), in_=x_scales[0, 4 * q : 4 * q + 4, :].bitcast(I32))
         nc.sync.dma_start(out=x_codes[:].bitcast(I32), in_=x_words[0].rearrange("p n t -> p (n t)").bitcast(I32))
         nc.sync.dma_start(lists[0][:], pos1)
         nc.sync.dma_start(out=w_raw[1][:], in_=w_view[:, :, P : 2 * P])
@@ -72,6 +71,7 @@ def tile_picked_wmedian_none_l_kernel(tc, x_words, x_scales, w1, pos1, pos2, pos
         project(0, 1)
         nc.scalar.copy(y[0][:, 0:HALF], acc[0][0][:])
         nc.vector.tensor_copy(y[0][:, HALF:T], acc[0][1][:])
+        w_bf.append(keep.tile([P, P, PACK], BF16, name="w_bf1", tag="relay", align_bytes=64))
         nc.scalar.copy(w_bf[1][:], w_raw[1][:].rearrange("p j n -> p n j"))
         gather(0, 0, 0)
         gather(0, 0, 1)

@@ -39,7 +39,8 @@ def tile_picked_wmedian_none_l_kernel(tc, x_words, x_scales, w1, pos1, pos2, pos
         lo = [keep.tile([P, T], F32, name=f"lo{b}") for b in range(2)]
         cut = [keep.tile([P, T], F32, name=f"cut{b}") for b in range(2)]
         med = [keep.tile([P, T], F32, name=f"med{b}") for b in range(2)]
-        acc = [[psum.tile([P, HALF], F32, name=f"acc{b}_{h}") for h in range(2)] for b in range(2)]
+        widths = [T // 4, HALF]
+        acc = [[psum.tile([P, widths[b]], F32, name=f"acc{b}_{h}") for h in range(T // widths[b])] for b in range(2)]
 
         w_view = w1.rearrange("(p j) n -> p j n", j=PACK)
         nc.sync.dma_start(out=w_raw[0][:], in_=w_view[:, :, 0:P])
@@ -55,7 +56,7 @@ def tile_picked_wmedian_none_l_kernel(tc, x_words, x_scales, w1, pos1, pos2, pos
             nc.vector.quantize_mx(out=w_codes[b][:].bitcast(FP8X4), scales=w_sc[b][:], in_=w_bf[b][:].rearrange("p n j -> p (n j)"))
 
         def project(b, h):
-            cols = slice(h * HALF, (h + 1) * HALF)
+            cols = slice(h * widths[b], (h + 1) * widths[b])
             nc.tensor.matmul_mx(out=acc[b][h][:], lhsT=w_codes[b][:].bitcast(FP8X4), lhsT_scale=w_sc[b][:],
                                 rhs=x_codes[:, cols].bitcast(FP8X4), rhs_scale=x_sc[:, cols], start=True, stop=True)
 
@@ -65,12 +66,20 @@ def tile_picked_wmedian_none_l_kernel(tc, x_words, x_scales, w1, pos1, pos2, pos
         def op(dst, a, c, alu, lo_col, hi_col):
             nc.vector.tensor_tensor(dst[:, lo_col:hi_col], a[:, lo_col:hi_col], c[:, lo_col:hi_col], alu)
 
-        nc.vector.tensor_copy(out=w_bf[0][:], in_=w_raw[0][:].rearrange("p j n -> p n j"))
-        quantise(0)
-        project(0, 0)
-        project(0, 1)
-        nc.scalar.copy(y[0][:, 0:HALF], acc[0][0][:])
-        nc.vector.tensor_copy(y[0][:, HALF:T], acc[0][1][:])
+        for c in range(2):
+            cols = slice(c * 64, (c + 1) * 64)
+            nc.vector.tensor_copy(out=w_bf[0][:, cols, :], in_=w_raw[0][:, :, cols].rearrange("p j n -> p n j"))
+        for c in range(2):
+            cols = slice(c * 64, (c + 1) * 64)
+            nc.vector.quantize_mx(out=w_codes[0][:, cols].bitcast(FP8X4), scales=w_sc[0][:, cols], in_=w_bf[0][:, cols, :].rearrange("p n j -> p (n j)"))
+        for h in range(4):
+            project(0, h)
+        for h in range(4):
+            cols = slice(h * widths[0], (h + 1) * widths[0])
+            if h % 2 == 0:
+                nc.scalar.copy(y[0][:, cols], acc[0][h][:])
+            else:
+                nc.vector.tensor_copy(y[0][:, cols], acc[0][h][:])
         w_bf.append(keep.tile([P, P, PACK], BF16, name="w_bf1", tag="relay", align_bytes=64))
         nc.scalar.copy(w_bf[1][:], w_raw[1][:].rearrange("p j n -> p n j"))
         gather(0, 0, 0)

@@ -18,6 +18,7 @@ MIN = mybir.AluOpType.min
 P = 128
 PACK = 4
 HALF = T // 2
+WINDOW = 704
 
 
 def tile_picked_wmedian_none_l_kernel(tc, x_words, x_scales, w1, pos1, pos2, pos3, out):
@@ -33,13 +34,13 @@ def tile_picked_wmedian_none_l_kernel(tc, x_words, x_scales, w1, pos1, pos2, pos
         w_sc = [keep.tile([P, P], U8, name=f"w_sc{b}", align_bytes=64) for b in range(2)]
         x_codes = keep.tile([P, T], U32, name="x_codes", align_bytes=64)
         x_sc = keep.tile([P, T], U8, name="x_sc", align_bytes=64)
-        y = [keep.tile([P, T], F32, name=f"y{b}") for b in range(2)]
+        y = [keep.tile([P, WINDOW], F32, name=f"y{b}") for b in range(2)]
         picked = [[keep.tile([P, T], F32, name=f"n{b}_{i}") for i in range(3)] for b in range(2)]
         hi = [keep.tile([P, T], F32, name=f"hi{b}") for b in range(2)]
         lo = [keep.tile([P, T], F32, name=f"lo{b}") for b in range(2)]
         cut = [keep.tile([P, T], F32, name=f"cut{b}") for b in range(2)]
         med = [keep.tile([P, T], F32, name=f"med{b}") for b in range(2)]
-        widths = [T // 4, HALF]
+        widths = [T // 4, T // 4]
         acc = [[psum.tile([P, widths[b]], F32, name=f"acc{b}_{h}") for h in range(T // widths[b])] for b in range(2)]
 
         w_view = w1.rearrange("(p j) n -> p j n", j=PACK)
@@ -63,6 +64,9 @@ def tile_picked_wmedian_none_l_kernel(tc, x_words, x_scales, w1, pos1, pos2, pos
         def gather(b, i, h):
             nc.vector.tensor_copy(picked[b][i][:, h * HALF : (h + 1) * HALF], y[b][:].indirect(lists[i][:, h * 16 : (h + 1) * 16]))
 
+        def gather_all(b, i):
+            nc.vector.tensor_copy(picked[b][i][:], y[b][:].indirect(lists[i][:]))
+
         def op(dst, a, c, alu, lo_col, hi_col):
             nc.vector.tensor_tensor(dst[:, lo_col:hi_col], a[:, lo_col:hi_col], c[:, lo_col:hi_col], alu)
 
@@ -82,26 +86,22 @@ def tile_picked_wmedian_none_l_kernel(tc, x_words, x_scales, w1, pos1, pos2, pos
                 nc.vector.tensor_copy(y[0][:, cols], acc[0][h][:])
         w_bf.append(keep.tile([P, P, PACK], BF16, name="w_bf1", tag="relay", align_bytes=64))
         nc.scalar.copy(w_bf[1][:], w_raw[1][:].rearrange("p j n -> p n j"))
-        gather(0, 0, 0)
-        gather(0, 0, 1)
+        gather_all(0, 0)
         quantise(1)
-        project(1, 0)
-        project(1, 1)
-        nc.scalar.copy(y[1][:, 0:HALF], acc[1][0][:])
-        nc.scalar.copy(y[1][:, HALF:T], acc[1][1][:])
-        for i in (1, 2):
-            gather(0, i, 0)
-            gather(0, i, 1)
+        for h in range(4):
+            project(1, h)
+        for h in range(4):
+            nc.scalar.copy(y[1][:, h * widths[1] : (h + 1) * widths[1]], acc[1][h][:])
+        gather_all(0, 1)
+        gather_all(0, 2)
         op(hi[0], picked[0][0], picked[0][1], MAX, 0, T)
         op(lo[0], picked[0][0], picked[0][1], MIN, 0, T)
         op(cut[0], hi[0], picked[0][2], MIN, 0, T)
-        gather(1, 0, 0)
+        gather_all(1, 0)
         op(med[0], lo[0], cut[0], MAX, 0, T)
         nc.sync.dma_start(out=out[0:P, :], in_=med[0][:])
-        gather(1, 0, 1)
-        for i in (1, 2):
-            gather(1, i, 0)
-            gather(1, i, 1)
+        gather_all(1, 1)
+        gather_all(1, 2)
         op(hi[1], picked[1][0], picked[1][1], MAX, 0, T)
         op(lo[1], picked[1][0], picked[1][1], MIN, 0, T)
         op(cut[1], hi[1], picked[1][2], MIN, 0, HALF)

@@ -45,9 +45,9 @@ def tile_picked_wmedian_none_l_kernel(tc, x_words, x_scales, w1, pos1, pos2, pos
 
         w_view = w1.rearrange("(p j) n -> p j n", j=PACK)
         nc.sync.dma_start(out=w_raw[0][:], in_=w_view[:, :, 0:P])
-        for q in range(4):
-            nc.sync.dma_start(out=x_sc[32 * q : 32 * q + 4, :].bitcast(I32), in_=x_scales[0, 4 * q : 4 * q + 4, :].bitcast(I32))
         nc.sync.dma_start(out=x_codes[:].bitcast(I32), in_=x_words[0].rearrange("p n t -> p (n t)").bitcast(I32))
+        for q, queue in enumerate((nc.scalar, nc.scalar, nc.scalar, nc.sync)):
+            queue.dma_start(out=x_sc[32 * q : 32 * q + 4, :].bitcast(I32), in_=x_scales[0, 4 * q : 4 * q + 4, :].bitcast(I32))
         nc.sync.dma_start(lists[0][:], pos1)
         nc.sync.dma_start(out=w_raw[1][:], in_=w_view[:, :, P : 2 * P])
         nc.sync.dma_start(lists[1][:], pos2)
@@ -80,7 +80,7 @@ def tile_picked_wmedian_none_l_kernel(tc, x_words, x_scales, w1, pos1, pos2, pos
             project(0, h)
         for h in range(4):
             cols = slice(h * widths[0], (h + 1) * widths[0])
-            if h % 2 == 0:
+            if h % 2 == 1:
                 nc.scalar.copy(y[0][:, cols], acc[0][h][:])
             else:
                 nc.vector.tensor_copy(y[0][:, cols], acc[0][h][:])

@@ -17,7 +17,12 @@ MIN = mybir.AluOpType.min
 
 P = 128
 PACK = 4
+GROUP = 16
+LINE = 4
+PIECES = 4
+PIECE = T // PIECES
 HALF = T // 2
+W_HALF = P // 2
 WINDOW = 704
 
 
@@ -27,10 +32,13 @@ def tile_picked_wmedian_none_l_kernel(tc, x_words, x_scales, w1, pos1, pos2, pos
         keep = ctx.enter_context(tc.tile_pool(name="keep", bufs=1))
         psum = ctx.enter_context(tc.psum_pool(name="psum", bufs=1))
 
-        lists = [keep.tile([P, T // 16], U16, name=f"list{i}") for i in range(3)]
+        lists = [keep.tile([P, T // GROUP], U16, name=f"list{i}") for i in range(3)]
         w_raw = [keep.tile([P, PACK, P], F32, name=f"w_raw{b}") for b in range(2)]
-        w_bf = [keep.tile([P, P, PACK], BF16, name="w_bf0", align_bytes=64)]
-        w_codes = [keep.tile([P, P], U32, name="w_codes0", tag="relay", align_bytes=64), keep.tile([P, P], U32, name="w_codes1", align_bytes=64)]
+        w_bf0 = keep.tile([P, P, PACK], BF16, name="w_bf0", align_bytes=64)
+        w_codes = [
+            keep.tile([P, P], U32, name="w_codes0", tag="relay", align_bytes=64),
+            keep.tile([P, P], U32, name="w_codes1", align_bytes=64),
+        ]
         w_sc = [keep.tile([P, P], U8, name=f"w_sc{b}", align_bytes=64) for b in range(2)]
         x_codes = keep.tile([P, T], U32, name="x_codes", align_bytes=64)
         x_sc = keep.tile([P, T], U8, name="x_sc", align_bytes=64)
@@ -40,73 +48,82 @@ def tile_picked_wmedian_none_l_kernel(tc, x_words, x_scales, w1, pos1, pos2, pos
         lo = [keep.tile([P, T], F32, name=f"lo{b}") for b in range(2)]
         cut = [keep.tile([P, T], F32, name=f"cut{b}") for b in range(2)]
         med = [keep.tile([P, T], F32, name=f"med{b}") for b in range(2)]
-        widths = [T // 4, T // 4]
-        acc = [[psum.tile([P, widths[b]], F32, name=f"acc{b}_{h}") for h in range(T // widths[b])] for b in range(2)]
+        acc = [[psum.tile([P, PIECE], F32, name=f"acc{b}_{h}") for h in range(PIECES)] for b in range(2)]
 
         w_view = w1.rearrange("(p j) n -> p j n", j=PACK)
         nc.sync.dma_start(out=w_raw[0][:], in_=w_view[:, :, 0:P])
-        nc.sync.dma_start(out=x_codes[:].bitcast(I32), in_=x_words[0].rearrange("p n t -> p (n t)").bitcast(I32))
         for q, queue in enumerate((nc.scalar, nc.scalar, nc.scalar, nc.sync)):
             queue.dma_start(out=x_sc[32 * q : 32 * q + 4, :].bitcast(I32), in_=x_scales[0, 4 * q : 4 * q + 4, :].bitcast(I32))
+        nc.sync.dma_start(out=x_codes[:].bitcast(I32), in_=x_words[0].rearrange("p n t -> p (n t)").bitcast(I32))
         nc.sync.dma_start(lists[0][:], pos1)
-        nc.sync.dma_start(out=w_raw[1][:], in_=w_view[:, :, P : 2 * P])
+        nc.sync.dma_start(out=w_raw[1][:], in_=w_view[:, :, P:N])
         nc.sync.dma_start(lists[1][:], pos2)
         nc.sync.dma_start(lists[2][:], pos3)
 
-        def quantise(b):
-            nc.vector.quantize_mx(out=w_codes[b][:].bitcast(FP8X4), scales=w_sc[b][:], in_=w_bf[b][:].rearrange("p n j -> p (n j)"))
+        def piece(h):
+            return slice(h * PIECE, (h + 1) * PIECE)
 
-        def project(b, h):
-            cols = slice(h * widths[b], (h + 1) * widths[b])
-            nc.tensor.matmul_mx(out=acc[b][h][:], lhsT=w_codes[b][:].bitcast(FP8X4), lhsT_scale=w_sc[b][:],
-                                rhs=x_codes[:, cols].bitcast(FP8X4), rhs_scale=x_sc[:, cols], start=True, stop=True)
+        def project(b):
+            for h in range(PIECES):
+                nc.tensor.matmul_mx(
+                    out=acc[b][h][:],
+                    lhsT=w_codes[b][:].bitcast(FP8X4),
+                    lhsT_scale=w_sc[b][:],
+                    rhs=x_codes[:, piece(h)].bitcast(FP8X4),
+                    rhs_scale=x_sc[:, piece(h)],
+                    start=True,
+                    stop=True,
+                )
 
-        def gather(b, i, h):
-            nc.vector.tensor_copy(picked[b][i][:, h * HALF : (h + 1) * HALF], y[b][:].indirect(lists[i][:, h * 16 : (h + 1) * 16]))
-
-        def gather_all(b, i):
+        def gather(b, i):
             nc.vector.tensor_copy(picked[b][i][:], y[b][:].indirect(lists[i][:]))
 
-        def op(dst, a, c, alu, lo_col, hi_col):
-            nc.vector.tensor_tensor(dst[:, lo_col:hi_col], a[:, lo_col:hi_col], c[:, lo_col:hi_col], alu)
+        def combine(dst, first, second, alu, cols):
+            nc.vector.tensor_tensor(dst[:, cols], first[:, cols], second[:, cols], alu)
 
-        for c in range(2):
-            cols = slice(c * 64, (c + 1) * 64)
-            nc.vector.tensor_copy(out=w_bf[0][:, cols, :], in_=w_raw[0][:, :, cols].rearrange("p j n -> p n j"))
-        for c in range(2):
-            cols = slice(c * 64, (c + 1) * 64)
-            nc.vector.quantize_mx(out=w_codes[0][:, cols].bitcast(FP8X4), scales=w_sc[0][:, cols], in_=w_bf[0][:, cols, :].rearrange("p n j -> p (n j)"))
-        for h in range(4):
-            project(0, h)
-        for h in range(4):
-            cols = slice(h * widths[0], (h + 1) * widths[0])
-            if h % 2 == 1:
-                nc.scalar.copy(y[0][:, cols], acc[0][h][:])
+        w_halves = [slice(0, W_HALF), slice(W_HALF, P)]
+        for cols in w_halves:
+            nc.vector.tensor_copy(
+                out=w_bf0[:, cols, :].rearrange("p (c i) j -> p c j i", i=LINE),
+                in_=w_raw[0][:, :, cols].rearrange("p j (c i) -> p c j i", i=LINE),
+            )
+        for cols in w_halves:
+            nc.vector.quantize_mx(
+                out=w_codes[0][:, cols].bitcast(FP8X4),
+                scales=w_sc[0][:, cols],
+                in_=w_bf0[:, cols, :].rearrange("p n j -> p (n j)"),
+            )
+        project(0)
+        for h in range(PIECES):
+            if h % 2 == 0:
+                nc.vector.tensor_copy(y[0][:, piece(h)], acc[0][h][:])
             else:
-                nc.vector.tensor_copy(y[0][:, cols], acc[0][h][:])
-        w_bf.append(keep.tile([P, P, PACK], BF16, name="w_bf1", tag="relay", align_bytes=64))
-        nc.scalar.copy(w_bf[1][:], w_raw[1][:].rearrange("p j n -> p n j"))
-        gather_all(0, 0)
-        quantise(1)
-        for h in range(4):
-            project(1, h)
-        for h in range(4):
-            nc.scalar.copy(y[1][:, h * widths[1] : (h + 1) * widths[1]], acc[1][h][:])
-        gather_all(0, 1)
-        gather_all(0, 2)
-        op(hi[0], picked[0][0], picked[0][1], MAX, 0, T)
-        op(lo[0], picked[0][0], picked[0][1], MIN, 0, T)
-        op(cut[0], hi[0], picked[0][2], MIN, 0, T)
-        gather_all(1, 0)
-        op(med[0], lo[0], cut[0], MAX, 0, T)
+                nc.scalar.copy(y[0][:, piece(h)], acc[0][h][:])
+
+        w_bf1 = keep.tile([P, P, PACK], BF16, name="w_bf1", tag="relay", align_bytes=64)
+        nc.scalar.copy(w_bf1[:], w_raw[1][:].rearrange("p j n -> p n j"))
+        gather(0, 0)
+        nc.vector.quantize_mx(out=w_codes[1][:].bitcast(FP8X4), scales=w_sc[1][:], in_=w_bf1[:].rearrange("p n j -> p (n j)"))
+        project(1)
+        for h in range(PIECES):
+            nc.scalar.copy(y[1][:, piece(h)], acc[1][h][:])
+
+        whole = slice(0, T)
+        gather(0, 1)
+        gather(0, 2)
+        combine(hi[0], picked[0][0], picked[0][1], MAX, whole)
+        combine(lo[0], picked[0][0], picked[0][1], MIN, whole)
+        combine(cut[0], hi[0], picked[0][2], MIN, whole)
+        gather(1, 0)
+        combine(med[0], lo[0], cut[0], MAX, whole)
         nc.sync.dma_start(out=out[0:P, :], in_=med[0][:])
-        gather_all(1, 1)
-        gather_all(1, 2)
-        op(hi[1], picked[1][0], picked[1][1], MAX, 0, T)
-        op(lo[1], picked[1][0], picked[1][1], MIN, 0, T)
-        op(cut[1], hi[1], picked[1][2], MIN, 0, HALF)
-        op(cut[1], hi[1], picked[1][2], MIN, HALF, T)
-        op(med[1], lo[1], cut[1], MAX, 0, HALF)
-        nc.sync.dma_start(out=out[P : 2 * P, 0:HALF], in_=med[1][:, 0:HALF])
-        op(med[1], lo[1], cut[1], MAX, HALF, T)
-        nc.scalar.dma_start(out=out[P : 2 * P, HALF:T], in_=med[1][:, HALF:T])
+
+        gather(1, 1)
+        gather(1, 2)
+        combine(hi[1], picked[1][0], picked[1][1], MAX, whole)
+        combine(lo[1], picked[1][0], picked[1][1], MIN, whole)
+        combine(cut[1], hi[1], picked[1][2], MIN, slice(0, HALF))
+        combine(cut[1], hi[1], picked[1][2], MIN, slice(HALF, T))
+        for h, queue in enumerate((nc.scalar, nc.sync, nc.scalar, nc.sync)):
+            combine(med[1], lo[1], cut[1], MAX, piece(h))
+            queue.dma_start(out=out[P:N, piece(h)], in_=med[1][:, piece(h)])

@@ -40,7 +40,7 @@ def tile_picked_wmedian_none_l_kernel(tc, x_words, x_scales, w1, pos1, pos2, pos
             keep.tile([P, P], U32, name="w_codes1", align_bytes=64),
         ]
         w_sc = [keep.tile([P, P], U8, name=f"w_sc{b}", align_bytes=64) for b in range(2)]
-        x_codes = keep.tile([P, T], U32, name="x_codes", align_bytes=64)
+        x_codes = [keep.tile([P, HALF], U32, name=f"x_codes{u}", align_bytes=64) for u in range(2)]
         x_sc = keep.tile([P, T], U8, name="x_sc", align_bytes=64)
         y = [keep.tile([P, WINDOW], F32, name=f"y{b}") for b in range(2)]
         picked = [[keep.tile([P, T], F32, name=f"n{b}_{i}") for i in range(3)] for b in range(2)]
@@ -52,12 +52,14 @@ def tile_picked_wmedian_none_l_kernel(tc, x_words, x_scales, w1, pos1, pos2, pos
 
         w_view = w1.rearrange("(p j) n -> p j n", j=PACK)
         nc.sync.dma_start(out=w_raw[0][:], in_=w_view[:, :, 0:P])
-        for q, queue in enumerate((nc.scalar, nc.scalar, nc.scalar, nc.sync)):
-            queue.dma_start(out=x_sc[32 * q : 32 * q + 4, :].bitcast(I32), in_=x_scales[0, 4 * q : 4 * q + 4, :].bitcast(I32))
-        nc.sync.dma_start(out=x_codes[:].bitcast(I32), in_=x_words[0].rearrange("p n t -> p (n t)").bitcast(I32))
+        for q in range(4):
+            nc.sync.dma_start(out=x_sc[32 * q : 32 * q + 4, :].bitcast(I32), in_=x_scales[0, 4 * q : 4 * q + 4, :].bitcast(I32))
+        x_view = x_words[0].rearrange("p n t -> p (n t)").bitcast(I32)
+        for u in range(2):
+            nc.sync.dma_start(out=x_codes[u][:].bitcast(I32), in_=x_view[:, u * HALF : (u + 1) * HALF])
         nc.sync.dma_start(lists[0][:], pos1)
-        nc.sync.dma_start(out=w_raw[1][:], in_=w_view[:, :, P:N])
         nc.sync.dma_start(lists[1][:], pos2)
+        nc.sync.dma_start(out=w_raw[1][:], in_=w_view[:, :, P:N])
         nc.sync.dma_start(lists[2][:], pos3)
 
         def piece(h):
@@ -69,7 +71,7 @@ def tile_picked_wmedian_none_l_kernel(tc, x_words, x_scales, w1, pos1, pos2, pos
                     out=acc[b][h][:],
                     lhsT=w_codes[b][:].bitcast(FP8X4),
                     lhsT_scale=w_sc[b][:],
-                    rhs=x_codes[:, piece(h)].bitcast(FP8X4),
+                    rhs=x_codes[h // 2][:, piece(h % 2)].bitcast(FP8X4),
                     rhs_scale=x_sc[:, piece(h)],
                     start=True,
                     stop=True,

@@ -24,6 +24,7 @@ PIECE = T // PIECES
 HALF = T // 2
 W_HALF = P // 2
 WINDOW = 704
+COPY = mybir.ActivationFunctionType.Copy
 
 
 def tile_picked_wmedian_none_l_kernel(tc, x_words, x_scales, w1, pos1, pos2, pos3, out):
@@ -34,98 +35,109 @@ def tile_picked_wmedian_none_l_kernel(tc, x_words, x_scales, w1, pos1, pos2, pos
 
         lists = [keep.tile([P, T // GROUP], U16, name=f"list{i}") for i in range(3)]
         w_raw = [keep.tile([P, PACK, P], F32, name=f"w_raw{b}") for b in range(2)]
-        w_bf0 = keep.tile([P, P, PACK], BF16, name="w_bf0", align_bytes=64)
-        w_codes = [
-            keep.tile([P, P], U32, name="w_codes0", tag="relay", align_bytes=64),
-            keep.tile([P, P], U32, name="w_codes1", align_bytes=64),
-        ]
+        w_bf = [keep.tile([P, P, PACK], BF16, name=f"w_bf{b}", align_bytes=64) for b in range(2)]
+        w_codes = [keep.tile([P, P], U32, name=f"w_codes{b}", align_bytes=64) for b in range(2)]
         w_sc = [keep.tile([P, P], U8, name=f"w_sc{b}", align_bytes=64) for b in range(2)]
-        x_codes = [keep.tile([P, HALF], U32, name=f"x_codes{u}", align_bytes=64) for u in range(2)]
+        x_codes = keep.tile([P, T], U32, name="x_codes", align_bytes=64)
         x_sc = keep.tile([P, T], U8, name="x_sc", align_bytes=64)
         y = [keep.tile([P, WINDOW], F32, name=f"y{b}") for b in range(2)]
-        picked = [[keep.tile([P, T], F32, name=f"n{b}_{i}") for i in range(3)] for b in range(2)]
+        first = keep.tile([P, T], F32, name="first")
+        second = keep.tile([P, T], F32, name="second")
+        third = [keep.tile([P, T], F32, name=f"third{b}") for b in range(2)]
         hi = [keep.tile([P, T], F32, name=f"hi{b}") for b in range(2)]
         lo = [keep.tile([P, T], F32, name=f"lo{b}") for b in range(2)]
         cut = [keep.tile([P, T], F32, name=f"cut{b}") for b in range(2)]
         med = [keep.tile([P, T], F32, name=f"med{b}") for b in range(2)]
-        acc = [[psum.tile([P, PIECE], F32, name=f"acc{b}_{h}") for h in range(PIECES)] for b in range(2)]
+        acc0 = [psum.tile([P, PIECE], F32, name=f"acc0_{h}", tag=f"bank{h}") for h in range(PIECES)]
 
         w_view = w1.rearrange("(p j) n -> p j n", j=PACK)
         nc.sync.dma_start(out=w_raw[0][:], in_=w_view[:, :, 0:P])
         for q in range(4):
             nc.sync.dma_start(out=x_sc[32 * q : 32 * q + 4, :].bitcast(I32), in_=x_scales[0, 4 * q : 4 * q + 4, :].bitcast(I32))
-        x_view = x_words[0].rearrange("p n t -> p (n t)").bitcast(I32)
-        for u in range(2):
-            nc.sync.dma_start(out=x_codes[u][:].bitcast(I32), in_=x_view[:, u * HALF : (u + 1) * HALF])
-        nc.sync.dma_start(lists[0][:], pos1)
-        nc.sync.dma_start(lists[1][:], pos2)
+        nc.sync.dma_start(out=x_codes[:].bitcast(I32), in_=x_words[0].rearrange("p n t -> p (n t)").bitcast(I32))
         nc.sync.dma_start(out=w_raw[1][:], in_=w_view[:, :, P:N])
-        nc.sync.dma_start(lists[2][:], pos3)
+        for tile, pos in zip(lists, (pos1, pos2, pos3)):
+            nc.sync.dma_start(tile[:], pos)
 
         def piece(h):
             return slice(h * PIECE, (h + 1) * PIECE)
 
-        def project(b):
-            for h in range(PIECES):
-                nc.tensor.matmul_mx(
-                    out=acc[b][h][:],
-                    lhsT=w_codes[b][:].bitcast(FP8X4),
-                    lhsT_scale=w_sc[b][:],
-                    rhs=x_codes[h // 2][:, piece(h % 2)].bitcast(FP8X4),
-                    rhs_scale=x_sc[:, piece(h)],
-                    start=True,
-                    stop=True,
-                )
+        def half(u):
+            return slice(u * HALF, (u + 1) * HALF)
 
-        def gather(b, i):
-            nc.vector.tensor_copy(picked[b][i][:], y[b][:].indirect(lists[i][:]))
-
-        def combine(dst, first, second, alu, cols):
-            nc.vector.tensor_tensor(dst[:, cols], first[:, cols], second[:, cols], alu)
-
-        w_halves = [slice(0, W_HALF), slice(W_HALF, P)]
-        for cols in w_halves:
+        def cast(b, cols):
             nc.vector.tensor_copy(
-                out=w_bf0[:, cols, :].rearrange("p (c i) j -> p c j i", i=LINE),
-                in_=w_raw[0][:, :, cols].rearrange("p j (c i) -> p c j i", i=LINE),
+                out=w_bf[b][:, cols, :].rearrange("p (c i) j -> p c j i", i=LINE),
+                in_=w_raw[b][:, :, cols].rearrange("p j (c i) -> p c j i", i=LINE),
             )
-        for cols in w_halves:
-            nc.vector.quantize_mx(
-                out=w_codes[0][:, cols].bitcast(FP8X4),
-                scales=w_sc[0][:, cols],
-                in_=w_bf0[:, cols, :].rearrange("p n j -> p (n j)"),
-            )
-        project(0)
-        for h in range(PIECES):
-            if h % 2 == 0:
-                nc.vector.tensor_copy(y[0][:, piece(h)], acc[0][h][:])
-            else:
-                nc.scalar.copy(y[0][:, piece(h)], acc[0][h][:])
 
-        w_bf1 = keep.tile([P, P, PACK], BF16, name="w_bf1", tag="relay", align_bytes=64)
-        nc.scalar.copy(w_bf1[:], w_raw[1][:].rearrange("p j n -> p n j"))
-        gather(0, 0)
-        nc.vector.quantize_mx(out=w_codes[1][:].bitcast(FP8X4), scales=w_sc[1][:], in_=w_bf1[:].rearrange("p n j -> p (n j)"))
-        project(1)
-        for h in range(PIECES):
-            nc.scalar.copy(y[1][:, piece(h)], acc[1][h][:])
+        def quantise(b, cols):
+            nc.vector.quantize_mx(
+                out=w_codes[b][:, cols].bitcast(FP8X4),
+                scales=w_sc[b][:, cols],
+                in_=w_bf[b][:, cols, :].rearrange("p n j -> p (n j)"),
+            )
+
+        def project(b, acc, cols):
+            nc.tensor.matmul_mx(
+                out=acc[:],
+                lhsT=w_codes[b][:].bitcast(FP8X4),
+                lhsT_scale=w_sc[b][:],
+                rhs=x_codes[:, cols].bitcast(FP8X4),
+                rhs_scale=x_sc[:, cols],
+                start=True,
+                stop=True,
+            )
+
+        def window(b, i, cols):
+            return y[b][:].indirect(lists[i][:, cols.start // GROUP : cols.stop // GROUP])
+
+        def gather_vector(dst, b, i, cols):
+            nc.vector.tensor_copy(dst[:, cols], window(b, i, cols))
+
+        def gather_scalar(dst, b, i, cols):
+            nc.scalar.activation(dst[:, cols], window(b, i, cols), COPY)
+
+        def combine(dst, in0, in1, alu, cols):
+            nc.vector.tensor_tensor(dst[:, cols], in0[:, cols], in1[:, cols], alu)
 
         whole = slice(0, T)
-        gather(0, 1)
-        gather(0, 2)
-        combine(hi[0], picked[0][0], picked[0][1], MAX, whole)
-        combine(lo[0], picked[0][0], picked[0][1], MIN, whole)
-        combine(cut[0], hi[0], picked[0][2], MIN, whole)
-        gather(1, 0)
+        w_halves = [slice(0, W_HALF), slice(W_HALF, P)]
+        for b in range(2):
+            for cols in w_halves:
+                cast(b, cols)
+            for cols in w_halves:
+                quantise(b, cols)
+        for h in range(PIECES):
+            project(0, acc0[h], piece(h))
+            nc.scalar.activation(y[0][:, piece(h)], acc0[h][:], COPY)
+        acc1 = psum.tile([P, T], F32, name="acc1", tag=f"bank{PIECES - 1}")
+        project(1, acc1, whole)
+
+        gather_scalar(first, 0, 0, whole)
+        gather_vector(second, 0, 1, whole)
+        nc.scalar.activation(y[1][:, whole], acc1[:], COPY)
+        gather_scalar(third[0], 0, 2, half(0))
+        gather_vector(third[0], 0, 2, half(1))
+        gather_scalar(third[1], 1, 2, half(0))
+        combine(hi[0], first, second, MAX, whole)
+        combine(lo[0], first, second, MIN, whole)
+        combine(cut[0], hi[0], third[0], MIN, whole)
+        for u in range(2):
+            gather_scalar(first, 1, 0, half(u))
+            gather_scalar(second, 1, 1, half(u))
         combine(med[0], lo[0], cut[0], MAX, whole)
         nc.sync.dma_start(out=out[0:P, :], in_=med[0][:])
-
-        gather(1, 1)
-        gather(1, 2)
-        combine(hi[1], picked[1][0], picked[1][1], MAX, whole)
-        combine(lo[1], picked[1][0], picked[1][1], MIN, whole)
-        combine(cut[1], hi[1], picked[1][2], MIN, slice(0, HALF))
-        combine(cut[1], hi[1], picked[1][2], MIN, slice(HALF, T))
-        for h, queue in enumerate((nc.scalar, nc.sync, nc.scalar, nc.sync)):
+        gather_scalar(lo[0], 1, 2, half(1))
+        combine(hi[1], first, second, MAX, half(0))
+        combine(lo[1], first, second, MIN, half(0))
+        combine(cut[1], hi[1], third[1], MIN, half(0))
+        combine(hi[1], first, second, MAX, half(1))
+        combine(med[1], lo[1], cut[1], MAX, half(0))
+        nc.sync.dma_start(out=out[P:N, half(0)], in_=med[1][:, half(0)])
+        combine(lo[1], first, second, MIN, half(1))
+        combine(cut[1], hi[1], lo[0], MIN, piece(2))
+        combine(cut[1], hi[1], lo[0], MIN, piece(3))
+        for h, queue in ((2, nc.scalar), (3, nc.sync)):
             combine(med[1], lo[1], cut[1], MAX, piece(h))
             queue.dma_start(out=out[P:N, piece(h)], in_=med[1][:, piece(h)])

@@ -34,7 +34,7 @@ def tile_picked_wmedian_none_l_kernel(tc, x_words, x_scales, w1, pos1, pos2, pos
         psum = ctx.enter_context(tc.psum_pool(name="psum", bufs=1))
 
         lists = [keep.tile([P, T // GROUP], U16, name=f"list{i}") for i in range(3)]
-        w_raw = [keep.tile([P, PACK, P], F32, name=f"w_raw{b}") for b in range(2)]
+        w_raw = keep.tile([P, PACK, N], F32, name="w_raw")
         w_bf = [keep.tile([P, P, PACK], BF16, name=f"w_bf{b}", align_bytes=64) for b in range(2)]
         w_codes = [keep.tile([P, P], U32, name=f"w_codes{b}", align_bytes=64) for b in range(2)]
         w_sc = [keep.tile([P, P], U8, name=f"w_sc{b}", align_bytes=64) for b in range(2)]
@@ -43,6 +43,8 @@ def tile_picked_wmedian_none_l_kernel(tc, x_words, x_scales, w1, pos1, pos2, pos
         y = [keep.tile([P, WINDOW], F32, name=f"y{b}") for b in range(2)]
         first = keep.tile([P, T], F32, name="first")
         second = keep.tile([P, T], F32, name="second")
+        fourth = keep.tile([P, HALF], F32, name="fourth")
+        fifth = keep.tile([P, HALF], F32, name="fifth")
         third = [keep.tile([P, T], F32, name=f"third{b}") for b in range(2)]
         hi = [keep.tile([P, T], F32, name=f"hi{b}") for b in range(2)]
         lo = [keep.tile([P, T], F32, name=f"lo{b}") for b in range(2)]
@@ -50,12 +52,10 @@ def tile_picked_wmedian_none_l_kernel(tc, x_words, x_scales, w1, pos1, pos2, pos
         med = [keep.tile([P, T], F32, name=f"med{b}") for b in range(2)]
         acc0 = [psum.tile([P, PIECE], F32, name=f"acc0_{h}", tag=f"bank{h}") for h in range(PIECES)]
 
-        w_view = w1.rearrange("(p j) n -> p j n", j=PACK)
-        nc.sync.dma_start(out=w_raw[0][:], in_=w_view[:, :, 0:P])
+        nc.sync.dma_start(out=w_raw[:], in_=w1.rearrange("(p j) n -> p j n", j=PACK))
         for q in range(4):
             nc.sync.dma_start(out=x_sc[32 * q : 32 * q + 4, :].bitcast(I32), in_=x_scales[0, 4 * q : 4 * q + 4, :].bitcast(I32))
         nc.sync.dma_start(out=x_codes[:].bitcast(I32), in_=x_words[0].rearrange("p n t -> p (n t)").bitcast(I32))
-        nc.sync.dma_start(out=w_raw[1][:], in_=w_view[:, :, P:N])
         for tile, pos in zip(lists, (pos1, pos2, pos3)):
             nc.sync.dma_start(tile[:], pos)
 
@@ -65,10 +65,10 @@ def tile_picked_wmedian_none_l_kernel(tc, x_words, x_scales, w1, pos1, pos2, pos
         def half(u):
             return slice(u * HALF, (u + 1) * HALF)
 
-        def cast(b, cols):
+        def cast(cols):
             nc.vector.tensor_copy(
-                out=w_bf[b][:, cols, :].rearrange("p (c i) j -> p c j i", i=LINE),
-                in_=w_raw[b][:, :, cols].rearrange("p j (c i) -> p c j i", i=LINE),
+                out=w_bf[0][:, cols, :].rearrange("p (c i) j -> p c j i", i=LINE),
+                in_=w_raw[:, :, cols].rearrange("p j (c i) -> p c j i", i=LINE),
             )
 
         def quantise(b, cols):
@@ -103,11 +103,12 @@ def tile_picked_wmedian_none_l_kernel(tc, x_words, x_scales, w1, pos1, pos2, pos
 
         whole = slice(0, T)
         w_halves = [slice(0, W_HALF), slice(W_HALF, P)]
-        for b in range(2):
-            for cols in w_halves:
-                cast(b, cols)
-            for cols in w_halves:
-                quantise(b, cols)
+        for cols in w_halves:
+            cast(cols)
+        nc.scalar.copy(w_bf[1][:], w_raw[:, :, P:N].rearrange("p j n -> p n j"))
+        for cols in w_halves:
+            quantise(0, cols)
+        quantise(1, slice(0, P))
         for h in range(PIECES):
             project(0, acc0[h], piece(h))
             nc.scalar.activation(y[0][:, piece(h)], acc0[h][:], COPY)
@@ -116,21 +117,22 @@ def tile_picked_wmedian_none_l_kernel(tc, x_words, x_scales, w1, pos1, pos2, pos
 
         gather_scalar(first, 0, 0, whole)
         gather_vector(second, 0, 1, whole)
-        nc.scalar.activation(y[1][:, whole], acc1[:], COPY)
-        gather_scalar(third[0], 0, 2, half(0))
-        gather_vector(third[0], 0, 2, half(1))
-        gather_scalar(third[1], 1, 2, half(0))
+        nc.vector.tensor_copy(y[1][:, whole], acc1[:])
+        gather_scalar(third[0], 0, 2, whole)
+        gather_scalar(fourth, 1, 0, half(0))
+        gather_scalar(fifth, 1, 1, half(0))
+        gather_scalar(third[1], 1, 2, piece(1))
         combine(hi[0], first, second, MAX, whole)
         combine(lo[0], first, second, MIN, whole)
         combine(cut[0], hi[0], third[0], MIN, whole)
-        for u in range(2):
-            gather_scalar(first, 1, 0, half(u))
-            gather_scalar(second, 1, 1, half(u))
+        gather_scalar(first, 1, 0, half(1))
+        gather_scalar(second, 1, 1, half(1))
+        gather_vector(third[1], 1, 2, piece(0))
         combine(med[0], lo[0], cut[0], MAX, whole)
         nc.sync.dma_start(out=out[0:P, :], in_=med[0][:])
         gather_scalar(lo[0], 1, 2, half(1))
-        combine(hi[1], first, second, MAX, half(0))
-        combine(lo[1], first, second, MIN, half(0))
+        combine(hi[1], fourth, fifth, MAX, half(0))
+        combine(lo[1], fourth, fifth, MIN, half(0))
         combine(cut[1], hi[1], third[1], MIN, half(0))
         combine(hi[1], first, second, MAX, half(1))
         combine(med[1], lo[1], cut[1], MAX, half(0))

@@ -41,10 +41,8 @@ def tile_picked_wmedian_none_l_kernel(tc, x_words, x_scales, w1, pos1, pos2, pos
         x_codes = keep.tile([P, T], U32, name="x_codes", align_bytes=64)
         x_sc = keep.tile([P, T], U8, name="x_sc", align_bytes=64)
         y = [keep.tile([P, WINDOW], F32, name=f"y{b}") for b in range(2)]
-        first = keep.tile([P, T], F32, name="first")
-        second = keep.tile([P, T], F32, name="second")
-        fourth = keep.tile([P, HALF], F32, name="fourth")
-        fifth = keep.tile([P, HALF], F32, name="fifth")
+        first = [keep.tile([P, T], F32, name=f"first{b}") for b in range(2)]
+        second = [keep.tile([P, T], F32, name=f"second{b}") for b in range(2)]
         third = [keep.tile([P, T], F32, name=f"third{b}") for b in range(2)]
         hi = [keep.tile([P, T], F32, name=f"hi{b}") for b in range(2)]
         lo = [keep.tile([P, T], F32, name=f"lo{b}") for b in range(2)]
@@ -115,31 +113,24 @@ def tile_picked_wmedian_none_l_kernel(tc, x_words, x_scales, w1, pos1, pos2, pos
         acc1 = psum.tile([P, T], F32, name="acc1", tag=f"bank{PIECES - 1}")
         project(1, acc1, whole)
 
-        gather_scalar(first, 0, 0, whole)
-        gather_vector(second, 0, 1, whole)
+        gather_scalar(first[0], 0, 0, whole)
+        gather_vector(second[0], 0, 1, whole)
         nc.vector.tensor_copy(y[1][:, whole], acc1[:])
         gather_scalar(third[0], 0, 2, whole)
-        gather_scalar(fourth, 1, 0, half(0))
-        gather_scalar(fifth, 1, 1, half(0))
-        gather_scalar(third[1], 1, 2, piece(1))
-        combine(hi[0], first, second, MAX, whole)
-        combine(lo[0], first, second, MIN, whole)
+        gather_scalar(first[1], 1, 0, half(0))
+        gather_scalar(second[1], 1, 1, whole)
+        gather_scalar(third[1], 1, 2, half(0))
+        gather_scalar(third[1], 1, 2, half(1))
+        combine(hi[0], first[0], second[0], MAX, whole)
+        combine(lo[0], first[0], second[0], MIN, whole)
         combine(cut[0], hi[0], third[0], MIN, whole)
-        gather_scalar(first, 1, 0, half(1))
-        gather_scalar(second, 1, 1, half(1))
-        gather_vector(third[1], 1, 2, piece(0))
+        gather_vector(first[1], 1, 0, half(1))
         combine(med[0], lo[0], cut[0], MAX, whole)
         nc.sync.dma_start(out=out[0:P, :], in_=med[0][:])
-        gather_scalar(lo[0], 1, 2, half(1))
-        combine(hi[1], fourth, fifth, MAX, half(0))
-        combine(lo[1], fourth, fifth, MIN, half(0))
+        combine(hi[1], first[1], second[1], MAX, whole)
+        combine(lo[1], first[1], second[1], MIN, whole)
         combine(cut[1], hi[1], third[1], MIN, half(0))
-        combine(hi[1], first, second, MAX, half(1))
-        combine(med[1], lo[1], cut[1], MAX, half(0))
-        nc.sync.dma_start(out=out[P:N, half(0)], in_=med[1][:, half(0)])
-        combine(lo[1], first, second, MIN, half(1))
-        combine(cut[1], hi[1], lo[0], MIN, piece(2))
-        combine(cut[1], hi[1], lo[0], MIN, piece(3))
-        for h, queue in ((2, nc.scalar), (3, nc.sync)):
+        combine(cut[1], hi[1], third[1], MIN, half(1))
+        for h, queue in enumerate((nc.scalar, nc.sync, nc.scalar, nc.sync)):
             combine(med[1], lo[1], cut[1], MAX, piece(h))
             queue.dma_start(out=out[P:N, piece(h)], in_=med[1][:, piece(h)])

@@ -24,6 +24,7 @@ PIECE = T // PIECES
 HALF = T // 2
 W_HALF = P // 2
 WINDOW = 704
+SHARE = 224
 COPY = mybir.ActivationFunctionType.Copy
 
 
@@ -34,7 +35,7 @@ def tile_picked_wmedian_none_l_kernel(tc, x_words, x_scales, w1, pos1, pos2, pos
         psum = ctx.enter_context(tc.psum_pool(name="psum", bufs=1))
 
         lists = [keep.tile([P, T // GROUP], U16, name=f"list{i}") for i in range(3)]
-        w_raw = keep.tile([P, PACK, N], F32, name="w_raw")
+        w_raw = [keep.tile([P, PACK, P], F32, name=f"w_raw{b}") for b in range(2)]
         w_bf = [keep.tile([P, P, PACK], BF16, name=f"w_bf{b}", align_bytes=64) for b in range(2)]
         w_codes = [keep.tile([P, P], U32, name=f"w_codes{b}", align_bytes=64) for b in range(2)]
         w_sc = [keep.tile([P, P], U8, name=f"w_sc{b}", align_bytes=64) for b in range(2)]
@@ -50,10 +51,12 @@ def tile_picked_wmedian_none_l_kernel(tc, x_words, x_scales, w1, pos1, pos2, pos
         med = [keep.tile([P, T], F32, name=f"med{b}") for b in range(2)]
         acc0 = [psum.tile([P, PIECE], F32, name=f"acc0_{h}", tag=f"bank{h}") for h in range(PIECES)]
 
-        nc.sync.dma_start(out=w_raw[:], in_=w1.rearrange("(p j) n -> p j n", j=PACK))
+        w_view = w1.rearrange("(p j) n -> p j n", j=PACK)
+        nc.sync.dma_start(out=w_raw[0][:], in_=w_view[:, :, 0:P])
         for q in range(4):
             nc.sync.dma_start(out=x_sc[32 * q : 32 * q + 4, :].bitcast(I32), in_=x_scales[0, 4 * q : 4 * q + 4, :].bitcast(I32))
         nc.sync.dma_start(out=x_codes[:].bitcast(I32), in_=x_words[0].rearrange("p n t -> p (n t)").bitcast(I32))
+        nc.sync.dma_start(out=w_raw[1][:], in_=w_view[:, :, P:N])
         for tile, pos in zip(lists, (pos1, pos2, pos3)):
             nc.sync.dma_start(tile[:], pos)
 
@@ -63,10 +66,10 @@ def tile_picked_wmedian_none_l_kernel(tc, x_words, x_scales, w1, pos1, pos2, pos
         def half(u):
             return slice(u * HALF, (u + 1) * HALF)
 
-        def cast(cols):
+        def cast(b, cols):
             nc.vector.tensor_copy(
-                out=w_bf[0][:, cols, :].rearrange("p (c i) j -> p c j i", i=LINE),
-                in_=w_raw[:, :, cols].rearrange("p j (c i) -> p c j i", i=LINE),
+                out=w_bf[b][:, cols, :].rearrange("p (c i) j -> p c j i", i=LINE),
+                in_=w_raw[b][:, :, cols].rearrange("p j (c i) -> p c j i", i=LINE),
             )
 
         def quantise(b, cols):
@@ -101,12 +104,11 @@ def tile_picked_wmedian_none_l_kernel(tc, x_words, x_scales, w1, pos1, pos2, pos
 
         whole = slice(0, T)
         w_halves = [slice(0, W_HALF), slice(W_HALF, P)]
-        for cols in w_halves:
-            cast(cols)
-        nc.scalar.copy(w_bf[1][:], w_raw[:, :, P:N].rearrange("p j n -> p n j"))
-        for cols in w_halves:
-            quantise(0, cols)
-        quantise(1, slice(0, P))
+        for b in range(2):
+            for cols in w_halves:
+                cast(b, cols)
+            for cols in w_halves:
+                quantise(b, cols)
         for h in range(PIECES):
             project(0, acc0[h], piece(h))
             nc.scalar.activation(y[0][:, piece(h)], acc0[h][:], COPY)
@@ -117,14 +119,14 @@ def tile_picked_wmedian_none_l_kernel(tc, x_words, x_scales, w1, pos1, pos2, pos
         gather_vector(second[0], 0, 1, whole)
         nc.vector.tensor_copy(y[1][:, whole], acc1[:])
         gather_scalar(third[0], 0, 2, whole)
-        gather_scalar(first[1], 1, 0, half(0))
+        gather_scalar(first[1], 1, 0, slice(0, SHARE))
         gather_scalar(second[1], 1, 1, whole)
         gather_scalar(third[1], 1, 2, half(0))
         gather_scalar(third[1], 1, 2, half(1))
         combine(hi[0], first[0], second[0], MAX, whole)
         combine(lo[0], first[0], second[0], MIN, whole)
         combine(cut[0], hi[0], third[0], MIN, whole)
-        gather_vector(first[1], 1, 0, half(1))
+        gather_vector(first[1], 1, 0, slice(SHARE, T))
         combine(med[0], lo[0], cut[0], MAX, whole)
         nc.sync.dma_start(out=out[0:P, :], in_=med[0][:])
         combine(hi[1], first[1], second[1], MAX, whole)

@@ -112,12 +112,14 @@ def tile_picked_wmedian_none_l_kernel(tc, x_words, x_scales, w1, pos1, pos2, pos
         for h in range(PIECES):
             project(0, acc0[h], piece(h))
             nc.scalar.activation(y[0][:, piece(h)], acc0[h][:], COPY)
-        acc1 = psum.tile([P, T], F32, name="acc1", tag=f"bank{PIECES - 1}")
-        project(1, acc1, whole)
+        acc1 = [psum.tile([P, HALF], F32, name=f"acc1_{u}", tag=f"bank{PIECES - 2 + u}") for u in range(2)]
+        for u in range(2):
+            project(1, acc1[u], half(u))
 
-        gather_scalar(first[0], 0, 0, whole)
-        gather_vector(second[0], 0, 1, whole)
-        nc.vector.tensor_copy(y[1][:, whole], acc1[:])
+        gather_vector(first[0], 0, 0, whole)
+        gather_scalar(second[0], 0, 1, whole)
+        for u in range(2):
+            nc.vector.tensor_copy(y[1][:, half(u)], acc1[u][:])
         gather_scalar(third[0], 0, 2, whole)
         gather_scalar(first[1], 1, 0, slice(0, SHARE))
         gather_scalar(second[1], 1, 1, whole)

@@ -24,7 +24,7 @@ PIECE = T // PIECES
 HALF = T // 2
 W_HALF = P // 2
 WINDOW = 704
-SHARE = 224
+SHARE = 256
 COPY = mybir.ActivationFunctionType.Copy
 
 
@@ -104,14 +104,19 @@ def tile_picked_wmedian_none_l_kernel(tc, x_words, x_scales, w1, pos1, pos2, pos
 
         whole = slice(0, T)
         w_halves = [slice(0, W_HALF), slice(W_HALF, P)]
-        for b in range(2):
-            for cols in w_halves:
-                cast(b, cols)
-            for cols in w_halves:
-                quantise(b, cols)
+        for cols in w_halves:
+            cast(0, cols)
+        for cols in w_halves:
+            quantise(0, cols)
         for h in range(PIECES):
             project(0, acc0[h], piece(h))
-            nc.scalar.activation(y[0][:, piece(h)], acc0[h][:], COPY)
+        nc.vector.tensor_copy(y[0][:, piece(0)], acc0[0][:])
+        for h in range(1, PIECES):
+            nc.scalar.copy(y[0][:, piece(h)], acc0[h][:])
+        for cols in w_halves:
+            cast(1, cols)
+        for cols in w_halves:
+            quantise(1, cols)
         acc1 = [psum.tile([P, HALF], F32, name=f"acc1_{u}", tag=f"bank{PIECES - 2 + u}") for u in range(2)]
         for u in range(2):
             project(1, acc1[u], half(u))

@@ -24,7 +24,7 @@ PIECE = T // PIECES
 HALF = T // 2
 W_HALF = P // 2
 WINDOW = 704
-SHARE = 256
+SHARE = 288
 COPY = mybir.ActivationFunctionType.Copy
 
 

@@ -25,6 +25,8 @@ HALF = T // 2
 W_HALF = P // 2
 WINDOW = 704
 SHARE = 288
+REGION = 64 * 1024
+ROW = T * 4
 COPY = mybir.ActivationFunctionType.Copy
 
 
@@ -32,6 +34,7 @@ def tile_picked_wmedian_none_l_kernel(tc, x_words, x_scales, w1, pos1, pos2, pos
     nc = tc.nc
     with ExitStack() as ctx:
         keep = ctx.enter_context(tc.tile_pool(name="keep", bufs=1))
+        work = ctx.enter_context(tc.tile_pool(name="work", bufs=1))
         psum = ctx.enter_context(tc.psum_pool(name="psum", bufs=1))
 
         lists = [keep.tile([P, T // GROUP], U16, name=f"list{i}") for i in range(3)]
@@ -41,14 +44,14 @@ def tile_picked_wmedian_none_l_kernel(tc, x_words, x_scales, w1, pos1, pos2, pos
         w_sc = [keep.tile([P, P], U8, name=f"w_sc{b}", align_bytes=64) for b in range(2)]
         x_codes = keep.tile([P, T], U32, name="x_codes", align_bytes=64)
         x_sc = keep.tile([P, T], U8, name="x_sc", align_bytes=64)
-        y = [keep.tile([P, WINDOW], F32, name=f"y{b}") for b in range(2)]
-        first = [keep.tile([P, T], F32, name=f"first{b}") for b in range(2)]
-        second = [keep.tile([P, T], F32, name=f"second{b}") for b in range(2)]
-        third = [keep.tile([P, T], F32, name=f"third{b}") for b in range(2)]
-        hi = [keep.tile([P, T], F32, name=f"hi{b}") for b in range(2)]
-        lo = [keep.tile([P, T], F32, name=f"lo{b}") for b in range(2)]
-        cut = [keep.tile([P, T], F32, name=f"cut{b}") for b in range(2)]
-        med = [keep.tile([P, T], F32, name=f"med{b}") for b in range(2)]
+        y = [work.tile([P, WINDOW], F32, name=f"y{b}", offset=b * WINDOW * 4) for b in range(2)]
+        first = [work.tile([P, T], F32, name=f"first{b}", offset=1 * REGION + (0 + b) * ROW) for b in range(2)]
+        second = [work.tile([P, T], F32, name=f"second{b}", offset=1 * REGION + (2 + b) * ROW) for b in range(2)]
+        third = [work.tile([P, T], F32, name=f"third{b}", offset=1 * REGION + (4 + b) * ROW) for b in range(2)]
+        hi = [work.tile([P, T], F32, name=f"hi{b}", offset=2 * REGION + (0 + b) * ROW) for b in range(2)]
+        lo = [work.tile([P, T], F32, name=f"lo{b}", offset=2 * REGION + (2 + b) * ROW) for b in range(2)]
+        cut = [work.tile([P, T], F32, name=f"cut{b}", offset=2 * REGION + (4 + b) * ROW) for b in range(2)]
+        med = [work.tile([P, T], F32, name=f"med{b}", offset=2 * REGION + (6 + b) * ROW) for b in range(2)]
         acc0 = [psum.tile([P, PIECE], F32, name=f"acc0_{h}", tag=f"bank{h}") for h in range(PIECES)]
 
         w_view = w1.rearrange("(p j) n -> p j n", j=PACK)

@@ -24,7 +24,7 @@ PIECE = T // PIECES
 HALF = T // 2
 W_HALF = P // 2
 WINDOW = 704
-SHARE = 288
+SHARE = 192
 REGION = 64 * 1024
 ROW = T * 4
 COPY = mybir.ActivationFunctionType.Copy
@@ -124,25 +124,33 @@ def tile_picked_wmedian_none_l_kernel(tc, x_words, x_scales, w1, pos1, pos2, pos
         for u in range(2):
             project(1, acc1[u], half(u))
 
+        early, late = half(0), half(1)
         gather_vector(first[0], 0, 0, whole)
         gather_scalar(second[0], 0, 1, whole)
         for u in range(2):
             nc.vector.tensor_copy(y[1][:, half(u)], acc1[u][:])
         gather_scalar(third[0], 0, 2, whole)
-        gather_scalar(first[1], 1, 0, slice(0, SHARE))
-        gather_scalar(second[1], 1, 1, whole)
-        gather_scalar(third[1], 1, 2, half(0))
-        gather_scalar(third[1], 1, 2, half(1))
+        gather_scalar(first[1], 1, 0, slice(SHARE, T))
+        gather_scalar(second[1], 1, 1, early)
         combine(hi[0], first[0], second[0], MAX, whole)
         combine(lo[0], first[0], second[0], MIN, whole)
         combine(cut[0], hi[0], third[0], MIN, whole)
-        gather_vector(first[1], 1, 0, slice(SHARE, T))
+        second_late, third_last = third[0], hi[0]
+        gather_scalar(second_late, 1, 1, late)
+        gather_scalar(third_last, 1, 2, half(0))
+        gather_scalar(third_last, 1, 2, piece(2))
+        gather_scalar(third_last, 1, 2, piece(3))
+        gather_vector(first[1], 1, 0, slice(0, SHARE))
         combine(med[0], lo[0], cut[0], MAX, whole)
         nc.sync.dma_start(out=out[0:P, :], in_=med[0][:])
-        combine(hi[1], first[1], second[1], MAX, whole)
-        combine(lo[1], first[1], second[1], MIN, whole)
-        combine(cut[1], hi[1], third[1], MIN, half(0))
-        combine(cut[1], hi[1], third[1], MIN, half(1))
+        combine(hi[1], first[1], second[1], MAX, early)
+        combine(lo[1], first[1], second[1], MIN, early)
+        combine(hi[1], first[1], second_late, MAX, late)
+        combine(lo[1], first[1], second_late, MIN, late)
+        for h in range(PIECES - 1):
+            combine(cut[1], hi[1], third_last, MIN, piece(h))
         for h, queue in enumerate((nc.scalar, nc.sync, nc.scalar, nc.sync)):
             combine(med[1], lo[1], cut[1], MAX, piece(h))
             queue.dma_start(out=out[P:N, piece(h)], in_=med[1][:, piece(h)])
+            if h == 0:
+                combine(cut[1], hi[1], third_last, MIN, piece(3))

@@ -24,7 +24,7 @@ PIECE = T // PIECES
 HALF = T // 2
 W_HALF = P // 2
 WINDOW = 704
-SHARE = 192
+SHARE = 128
 REGION = 64 * 1024
 ROW = T * 4
 COPY = mybir.ActivationFunctionType.Copy

@@ -38,7 +38,8 @@ def tile_picked_wmedian_none_l_kernel(tc, x_words, x_scales, w1, pos1, pos2, pos
         psum = ctx.enter_context(tc.psum_pool(name="psum", bufs=1))
 
         lists = [keep.tile([P, T // GROUP], U16, name=f"list{i}") for i in range(3)]
-        w_raw = [keep.tile([P, PACK, P], F32, name=f"w_raw{b}") for b in range(2)]
+        w_pair = [keep.tile([P, 2, P], F32, name=f"w_pair{u}") for u in range(2)]
+        w_raw = keep.tile([P, PACK, P], F32, name="w_raw")
         w_bf = [keep.tile([P, P, PACK], BF16, name=f"w_bf{b}", align_bytes=64) for b in range(2)]
         w_codes = [keep.tile([P, P], U32, name=f"w_codes{b}", align_bytes=64) for b in range(2)]
         w_sc = [keep.tile([P, P], U8, name=f"w_sc{b}", align_bytes=64) for b in range(2)]
@@ -55,11 +56,12 @@ def tile_picked_wmedian_none_l_kernel(tc, x_words, x_scales, w1, pos1, pos2, pos
         acc0 = [psum.tile([P, PIECE], F32, name=f"acc0_{h}", tag=f"bank{h}") for h in range(PIECES)]
 
         w_view = w1.rearrange("(p j) n -> p j n", j=PACK)
-        nc.sync.dma_start(out=w_raw[0][:], in_=w_view[:, :, 0:P])
-        for q in range(4):
-            nc.sync.dma_start(out=x_sc[32 * q : 32 * q + 4, :].bitcast(I32), in_=x_scales[0, 4 * q : 4 * q + 4, :].bitcast(I32))
+        for u in range(2):
+            nc.sync.dma_start(out=w_pair[u][:], in_=w_view[:, 2 * u : 2 * u + 2, 0:P])
+        for q, queue in enumerate((nc.scalar, nc.scalar, nc.sync, nc.sync)):
+            queue.dma_start(out=x_sc[32 * q : 32 * q + 4, :].bitcast(I32), in_=x_scales[0, 4 * q : 4 * q + 4, :].bitcast(I32))
         nc.sync.dma_start(out=x_codes[:].bitcast(I32), in_=x_words[0].rearrange("p n t -> p (n t)").bitcast(I32))
-        nc.sync.dma_start(out=w_raw[1][:], in_=w_view[:, :, P:N])
+        nc.sync.dma_start(out=w_raw[:], in_=w_view[:, :, P:N])
         for tile, pos in zip(lists, (pos1, pos2, pos3)):
             nc.sync.dma_start(tile[:], pos)
 
@@ -69,10 +71,13 @@ def tile_picked_wmedian_none_l_kernel(tc, x_words, x_scales, w1, pos1, pos2, pos
         def half(u):
             return slice(u * HALF, (u + 1) * HALF)
 
-        def cast(b, cols):
+        def cast_pair(u, cols):
+            nc.vector.tensor_copy(out=w_bf[0][:, cols, 2 * u : 2 * u + 2], in_=w_pair[u][:, :, cols].rearrange("p j n -> p n j"))
+
+        def cast(cols):
             nc.vector.tensor_copy(
-                out=w_bf[b][:, cols, :].rearrange("p (c i) j -> p c j i", i=LINE),
-                in_=w_raw[b][:, :, cols].rearrange("p j (c i) -> p c j i", i=LINE),
+                out=w_bf[1][:, cols, :].rearrange("p (c i) j -> p c j i", i=LINE),
+                in_=w_raw[:, :, cols].rearrange("p j (c i) -> p c j i", i=LINE),
             )
 
         def quantise(b, cols):
@@ -107,8 +112,9 @@ def tile_picked_wmedian_none_l_kernel(tc, x_words, x_scales, w1, pos1, pos2, pos
 
         whole = slice(0, T)
         w_halves = [slice(0, W_HALF), slice(W_HALF, P)]
+        cast_pair(0, slice(0, P))
         for cols in w_halves:
-            cast(0, cols)
+            cast_pair(1, cols)
         for cols in w_halves:
             quantise(0, cols)
         for h in range(PIECES):
@@ -117,7 +123,7 @@ def tile_picked_wmedian_none_l_kernel(tc, x_words, x_scales, w1, pos1, pos2, pos
         for h in range(1, PIECES):
             nc.scalar.copy(y[0][:, piece(h)], acc0[h][:])
         for cols in w_halves:
-            cast(1, cols)
+            cast(cols)
         for cols in w_halves:
             quantise(1, cols)
         acc1 = [psum.tile([P, HALF], F32, name=f"acc1_{u}", tag=f"bank{PIECES - 2 + u}") for u in range(2)]
@@ -130,21 +136,22 @@ def tile_picked_wmedian_none_l_kernel(tc, x_words, x_scales, w1, pos1, pos2, pos
         for u in range(2):
             nc.vector.tensor_copy(y[1][:, half(u)], acc1[u][:])
         gather_scalar(third[0], 0, 2, whole)
-        gather_scalar(first[1], 1, 0, slice(SHARE, T))
-        gather_scalar(second[1], 1, 1, early)
+        gather_scalar(first[1], 1, 2, slice(SHARE, T))
         combine(hi[0], first[0], second[0], MAX, whole)
         combine(lo[0], first[0], second[0], MIN, whole)
+        second_early = second[0]
+        gather_scalar(second_early, 1, 1, early)
         combine(cut[0], hi[0], third[0], MIN, whole)
         second_late, third_last = third[0], hi[0]
         gather_scalar(second_late, 1, 1, late)
-        gather_scalar(third_last, 1, 2, half(0))
-        gather_scalar(third_last, 1, 2, piece(2))
-        gather_scalar(third_last, 1, 2, piece(3))
-        gather_vector(first[1], 1, 0, slice(0, SHARE))
+        gather_scalar(third_last, 1, 0, half(0))
+        gather_scalar(third_last, 1, 0, piece(2))
+        gather_scalar(third_last, 1, 0, piece(3))
+        gather_vector(first[1], 1, 2, slice(0, SHARE))
         combine(med[0], lo[0], cut[0], MAX, whole)
         nc.sync.dma_start(out=out[0:P, :], in_=med[0][:])
-        combine(hi[1], first[1], second[1], MAX, early)
-        combine(lo[1], first[1], second[1], MIN, early)
+        combine(hi[1], first[1], second_early, MAX, early)
+        combine(lo[1], first[1], second_early, MIN, early)
         combine(hi[1], first[1], second_late, MAX, late)
         combine(lo[1], first[1], second_late, MIN, late)
         for h in range(PIECES - 1):

@@ -58,7 +58,7 @@ def tile_picked_wmedian_none_l_kernel(tc, x_words, x_scales, w1, pos1, pos2, pos
         w_view = w1.rearrange("(p j) n -> p j n", j=PACK)
         for u in range(2):
             nc.sync.dma_start(out=w_pair[u][:], in_=w_view[:, 2 * u : 2 * u + 2, 0:P])
-        for q, queue in enumerate((nc.scalar, nc.scalar, nc.sync, nc.sync)):
+        for q, queue in enumerate((nc.scalar, nc.scalar, nc.scalar, nc.sync)):
             queue.dma_start(out=x_sc[32 * q : 32 * q + 4, :].bitcast(I32), in_=x_scales[0, 4 * q : 4 * q + 4, :].bitcast(I32))
         nc.sync.dma_start(out=x_codes[:].bitcast(I32), in_=x_words[0].rearrange("p n t -> p (n t)").bitcast(I32))
         nc.sync.dma_start(out=w_raw[:], in_=w_view[:, :, P:N])

@@ -119,8 +119,7 @@ def tile_picked_wmedian_none_l_kernel(tc, x_words, x_scales, w1, pos1, pos2, pos
             quantise(0, cols)
         for h in range(PIECES):
             project(0, acc0[h], piece(h))
-        nc.vector.tensor_copy(y[0][:, piece(0)], acc0[0][:])
-        for h in range(1, PIECES):
+        for h in range(PIECES):
             nc.scalar.copy(y[0][:, piece(h)], acc0[h][:])
         for cols in w_halves:
             cast(cols)

@@ -24,7 +24,7 @@ PIECE = T // PIECES
 HALF = T // 2
 W_HALF = P // 2
 WINDOW = 704
-SHARE = 128
+SHARE = 160
 REGION = 64 * 1024
 ROW = T * 4
 COPY = mybir.ActivationFunctionType.Copy
@@ -125,24 +125,22 @@ def tile_picked_wmedian_none_l_kernel(tc, x_words, x_scales, w1, pos1, pos2, pos
             cast(cols)
         for cols in w_halves:
             quantise(1, cols)
-        acc1 = [psum.tile([P, HALF], F32, name=f"acc1_{u}", tag=f"bank{PIECES - 2 + u}") for u in range(2)]
-        for u in range(2):
-            project(1, acc1[u], half(u))
+        acc1 = psum.tile([P, T], F32, name="acc1", tag=f"bank{PIECES - 1}")
+        project(1, acc1, whole)
 
         early, late = half(0), half(1)
         gather_vector(first[0], 0, 0, whole)
         gather_scalar(second[0], 0, 1, whole)
-        for u in range(2):
-            nc.vector.tensor_copy(y[1][:, half(u)], acc1[u][:])
+        nc.vector.tensor_copy(y[1][:, whole], acc1[:])
         gather_scalar(third[0], 0, 2, whole)
         gather_scalar(first[1], 1, 2, slice(SHARE, T))
         combine(hi[0], first[0], second[0], MAX, whole)
         combine(lo[0], first[0], second[0], MIN, whole)
         second_early = second[0]
         gather_scalar(second_early, 1, 1, early)
+        gather_scalar(second_early, 1, 1, late)
         combine(cut[0], hi[0], third[0], MIN, whole)
-        second_late, third_last = third[0], hi[0]
-        gather_scalar(second_late, 1, 1, late)
+        third_last = hi[0]
         gather_scalar(third_last, 1, 0, half(0))
         gather_scalar(third_last, 1, 0, piece(2))
         gather_scalar(third_last, 1, 0, piece(3))
@@ -151,8 +149,8 @@ def tile_picked_wmedian_none_l_kernel(tc, x_words, x_scales, w1, pos1, pos2, pos
         nc.sync.dma_start(out=out[0:P, :], in_=med[0][:])
         combine(hi[1], first[1], second_early, MAX, early)
         combine(lo[1], first[1], second_early, MIN, early)
-        combine(hi[1], first[1], second_late, MAX, late)
-        combine(lo[1], first[1], second_late, MIN, late)
+        combine(hi[1], first[1], second_early, MAX, late)
+        combine(lo[1], first[1], second_early, MIN, late)
         for h in range(PIECES - 1):
             combine(cut[1], hi[1], third_last, MIN, piece(h))
         for h, queue in enumerate((nc.scalar, nc.sync, nc.scalar, nc.sync)):

from contextlib import ExitStack

import concourse.mybir as mybir

K, T, N = 512, 512, 256
FLOPS = 2 * K * T * N

F32 = mybir.dt.float32
BF16 = mybir.dt.bfloat16
I32 = mybir.dt.int32
U32 = mybir.dt.uint32
U16 = mybir.dt.uint16
U8 = mybir.dt.uint8
FP8X4 = mybir.dt.float8_e4m3fn_x4
MAX = mybir.AluOpType.max
MIN = mybir.AluOpType.min

P = 128
PACK = 4
GROUP = 16
LINE = 4
PIECES = 4
PIECE = T // PIECES
HALF = T // 2
W_HALF = P // 2
WINDOW = 704
SHARE = 160
REGION = 64 * 1024
ROW = T * 4
COPY = mybir.ActivationFunctionType.Copy


def tile_picked_wmedian_none_l_kernel(tc, x_words, x_scales, w1, pos1, pos2, pos3, out):
    nc = tc.nc
    with ExitStack() as ctx:
        keep = ctx.enter_context(tc.tile_pool(name="keep", bufs=1))
        work = ctx.enter_context(tc.tile_pool(name="work", bufs=1))
        psum = ctx.enter_context(tc.psum_pool(name="psum", bufs=1))

        lists = [keep.tile([P, T // GROUP], U16, name=f"list{i}") for i in range(3)]
        w_pair = [keep.tile([P, 2, P], F32, name=f"w_pair{u}") for u in range(2)]
        w_raw = keep.tile([P, PACK, P], F32, name="w_raw")
        w_bf = [keep.tile([P, P, PACK], BF16, name=f"w_bf{b}", align_bytes=64) for b in range(2)]
        w_codes = [keep.tile([P, P], U32, name=f"w_codes{b}", align_bytes=64) for b in range(2)]
        w_sc = [keep.tile([P, P], U8, name=f"w_sc{b}", align_bytes=64) for b in range(2)]
        x_codes = keep.tile([P, T], U32, name="x_codes", align_bytes=64)
        x_sc = keep.tile([P, T], U8, name="x_sc", align_bytes=64)
        y = [work.tile([P, WINDOW], F32, name=f"y{b}", offset=b * WINDOW * 4) for b in range(2)]
        first = [work.tile([P, T], F32, name=f"first{b}", offset=1 * REGION + (0 + b) * ROW) for b in range(2)]
        second = [work.tile([P, T], F32, name=f"second{b}", offset=1 * REGION + (2 + b) * ROW) for b in range(2)]
        third = [work.tile([P, T], F32, name=f"third{b}", offset=1 * REGION + (4 + b) * ROW) for b in range(2)]
        hi = [work.tile([P, T], F32, name=f"hi{b}", offset=2 * REGION + (0 + b) * ROW) for b in range(2)]
        lo = [work.tile([P, T], F32, name=f"lo{b}", offset=2 * REGION + (2 + b) * ROW) for b in range(2)]
        cut = [work.tile([P, T], F32, name=f"cut{b}", offset=2 * REGION + (4 + b) * ROW) for b in range(2)]
        med = [work.tile([P, T], F32, name=f"med{b}", offset=2 * REGION + (6 + b) * ROW) for b in range(2)]
        acc0 = [psum.tile([P, PIECE], F32, name=f"acc0_{h}", tag=f"bank{h}") for h in range(PIECES)]

        w_view = w1.rearrange("(p j) n -> p j n", j=PACK)
        for u in range(2):
            nc.sync.dma_start(out=w_pair[u][:], in_=w_view[:, 2 * u : 2 * u + 2, 0:P])
        for q, queue in enumerate((nc.scalar, nc.scalar, nc.scalar, nc.sync)):
            queue.dma_start(out=x_sc[32 * q : 32 * q + 4, :].bitcast(I32), in_=x_scales[0, 4 * q : 4 * q + 4, :].bitcast(I32))
        nc.sync.dma_start(out=x_codes[:].bitcast(I32), in_=x_words[0].rearrange("p n t -> p (n t)").bitcast(I32))
        nc.sync.dma_start(out=w_raw[:], in_=w_view[:, :, P:N])
        for tile, pos in zip(lists, (pos1, pos2, pos3)):
            nc.sync.dma_start(tile[:], pos)

        def piece(h):
            return slice(h * PIECE, (h + 1) * PIECE)

        def half(u):
            return slice(u * HALF, (u + 1) * HALF)

        def cast_pair(u, cols):
            nc.vector.tensor_copy(out=w_bf[0][:, cols, 2 * u : 2 * u + 2], in_=w_pair[u][:, :, cols].rearrange("p j n -> p n j"))

        def cast(cols):
            nc.vector.tensor_copy(
                out=w_bf[1][:, cols, :].rearrange("p (c i) j -> p c j i", i=LINE),
                in_=w_raw[:, :, cols].rearrange("p j (c i) -> p c j i", i=LINE),
            )

        def quantise(b, cols):
            nc.vector.quantize_mx(
                out=w_codes[b][:, cols].bitcast(FP8X4),
                scales=w_sc[b][:, cols],
                in_=w_bf[b][:, cols, :].rearrange("p n j -> p (n j)"),
            )

        def project(b, acc, cols):
            nc.tensor.matmul_mx(
                out=acc[:],
                lhsT=w_codes[b][:].bitcast(FP8X4),
                lhsT_scale=w_sc[b][:],
                rhs=x_codes[:, cols].bitcast(FP8X4),
                rhs_scale=x_sc[:, cols],
                start=True,
                stop=True,
            )

        def window(b, i, cols):
            return y[b][:].indirect(lists[i][:, cols.start // GROUP : cols.stop // GROUP])

        def gather_vector(dst, b, i, cols):
            nc.vector.tensor_copy(dst[:, cols], window(b, i, cols))

        def gather_scalar(dst, b, i, cols):
            nc.scalar.activation(dst[:, cols], window(b, i, cols), COPY)

        def combine(dst, in0, in1, alu, cols):
            nc.vector.tensor_tensor(dst[:, cols], in0[:, cols], in1[:, cols], alu)

        whole = slice(0, T)
        w_halves = [slice(0, W_HALF), slice(W_HALF, P)]
        cast_pair(0, slice(0, P))
        for cols in w_halves:
            cast_pair(1, cols)
        for cols in w_halves:
            quantise(0, cols)
        for h in range(PIECES):
            project(0, acc0[h], piece(h))
        for h in range(PIECES):
            nc.scalar.copy(y[0][:, piece(h)], acc0[h][:])
        for cols in w_halves:
            cast(cols)
        for cols in w_halves:
            quantise(1, cols)
        acc1 = psum.tile([P, T], F32, name="acc1", tag=f"bank{PIECES - 1}")
        project(1, acc1, whole)

        early, late = half(0), half(1)
        gather_vector(first[0], 0, 0, whole)
        gather_scalar(second[0], 0, 1, whole)
        nc.vector.tensor_copy(y[1][:, whole], acc1[:])
        gather_scalar(third[0], 0, 2, whole)
        gather_scalar(first[1], 1, 2, slice(SHARE, T))
        combine(hi[0], first[0], second[0], MAX, whole)
        combine(lo[0], first[0], second[0], MIN, whole)
        second_early = second[0]
        gather_scalar(second_early, 1, 1, early)
        gather_scalar(second_early, 1, 1, late)
        combine(cut[0], hi[0], third[0], MIN, whole)
        third_last = hi[0]
        gather_scalar(third_last, 1, 0, half(0))
        gather_scalar(third_last, 1, 0, piece(2))
        gather_scalar(third_last, 1, 0, piece(3))
        gather_vector(first[1], 1, 2, slice(0, SHARE))
        combine(med[0], lo[0], cut[0], MAX, whole)
        nc.sync.dma_start(out=out[0:P, :], in_=med[0][:])
        combine(hi[1], first[1], second_early, MAX, early)
        combine(lo[1], first[1], second_early, MIN, early)
        combine(hi[1], first[1], second_early, MAX, late)
        combine(lo[1], first[1], second_early, MIN, late)
        for h in range(PIECES - 1):
            combine(cut[1], hi[1], third_last, MIN, piece(h))
        for h, queue in enumerate((nc.scalar, nc.sync, nc.scalar, nc.sync)):
            combine(med[1], lo[1], cut[1], MAX, piece(h))
            queue.dma_start(out=out[P:N, piece(h)], in_=med[1][:, piece(h)])
            if h == 0:
                combine(cut[1], hi[1], third_last, MIN, piece(3))
